import numpy as np
import ml_dtypes


def mxq(x, axis, fmt="e4m3"):
    dtype, down = {"e4m3": (ml_dtypes.float8_e4m3fn, 7), "e5m2": (ml_dtypes.float8_e5m2, 14)}[fmt]
    v = np.moveaxis(np.asarray(x, np.float32).astype(ml_dtypes.bfloat16).astype(np.float64), axis, -1)
    blocks = v.reshape(v.shape[:-1] + (-1, 32))
    amax = np.abs(blocks).max(-1, keepdims=True)
    byte = np.maximum(np.where(amax > 0, np.frexp(amax)[1] - 1 + 127, 0) - down, 1)
    scale = np.exp2(byte - 127.0)
    codes = (blocks / scale).astype(np.float32).astype(dtype).astype(np.float64)
    return np.moveaxis((codes * scale).reshape(v.shape), -1, axis)


WIDE = False


def mx_kscale(k):
    if not WIDE:
        return np.ones(k)
    levels = np.array([30, -30])
    if k % 512:
        return np.exp2(np.random.permutation(np.resize(levels, k // 32))).repeat(32)
    a = np.empty((k // 512, 16))
    for p in range(k // 512):
        a[p, :8] = np.random.permutation(np.resize(levels, 8))
        for g in range(8):
            far = levels[np.abs(levels - a[p, g]) >= 10]
            a[p, g + 8] = far[np.random.randint(len(far))]
    return np.exp2(a.ravel()).repeat(32)


def f64(x):
    return np.asarray(x).astype(np.float64)


def striped(idx):
    return np.tile(np.asarray(idx).reshape(-1, 16).T, (8, 1)).astype(np.uint16)


def unstriped(offs):
    return offs[:16].T.reshape(-1).astype(np.int64)


E2M1 = np.array([0.0, 0.5, 1.0, 1.5, 2.0, 3.0, 4.0, 6.0, -0.0, -0.5, -1.0, -1.5, -2.0, -3.0, -4.0, -6.0])


def pack_weight(w, fmt):
    k, n = w.shape
    w = f64(np.asarray(w, np.float32).astype(ml_dtypes.bfloat16)).reshape(k // 32, 32, n)
    amax = np.abs(w).max(1)
    if fmt in ("e4m3", "e5m2"):
        byte = np.frexp(amax)[1] - 1 + 127 - (7 if fmt == "e4m3" else 14)
    else:
        mant, ex = np.frexp(amax / 6.0)
        byte = np.where(mant > 0.5, ex, ex - 1) + 127
    byte = np.clip(np.where(amax > 0, byte, 1), 1, 254)
    scaled = (w * np.exp2(127.0 - byte)[:, None, :]).reshape(k, n).astype(np.float32)
    by_word = np.ascontiguousarray(scaled.reshape(k // 512, 128, 4, n).transpose(0, 1, 3, 2))
    if fmt in ("e4m3", "e5m2"):
        words = by_word.astype(ml_dtypes.float8_e4m3fn if fmt == "e4m3" else ml_dtypes.float8_e5m2).view(np.uint8)
    else:
        c = by_word.astype(ml_dtypes.float4_e2m1fn).view(np.uint8) & 0xF
        words = (c[..., 0::2] | (c[..., 1::2] << 4)).reshape(k // 512, 128, 2 * n)
    return np.ascontiguousarray(words), np.ascontiguousarray(byte.astype(np.uint8).reshape(k // 512, 16, n))


def unpack_weight(words, scales, fmt):
    g, _, n = scales.shape
    words = np.ascontiguousarray(words).reshape(g, 128, n, -1)
    if fmt in ("e4m3", "e5m2"):
        vals = words.view(ml_dtypes.float8_e4m3fn if fmt == "e4m3" else ml_dtypes.float8_e5m2).astype(np.float64)
    else:
        nib = np.empty((g, 128, n, 4), np.uint8)
        nib[..., 0::2] = words & 0xF
        nib[..., 1::2] = words >> 4
        vals = E2M1[nib]
    vals = vals * np.repeat(np.exp2(scales.astype(np.float64) - 127.0), 8, axis=1)[..., None]
    return vals.transpose(0, 1, 3, 2).reshape(g * 512, n)


def sigmoid(v):
    return 1.0 / (1.0 + np.exp(-v))


K, T, J, R, O, N, L, E = 512, 2048, 256, 512, 128, 256, 512, 1024


def setup_inputs():
    n = np.random.standard_normal
    idx = np.random.permutation(T)[:J]
    idx2 = np.random.permutation(T)[:J]
    idx3 = np.random.permutation(J)[:O]
    idx4 = np.random.permutation(J)[:O]
    idx5 = np.random.permutation(E)[:O]
    fk = mx_kscale(K)
    fr = mx_kscale(R)
    fl = mx_kscale(L)
    xtp = pack_weight(n((K, T)) / fk[:, None], "e2m1")
    wp = pack_weight(n((K, R)) * 1 / np.sqrt(K) * fk[:, None], "e5m2")
    w2p = pack_weight(n((K, R)) * 1 / np.sqrt(K) * fk[:, None] * fr, "e4m3")
    wbp = pack_weight(n((R, N)) * 1 / np.sqrt(R) / fr[:, None], "e4m3")
    sxp = pack_weight(n((L, O)) / fl[:, None], "e5m2")
    wsp = pack_weight(n((L, N)) * 1 / np.sqrt(L) * fl[:, None], "e4m3")
    return {
        "xt_words": xtp[0],
        "xt_scales": xtp[1],
        "w_words": wp[0],
        "w_scales": wp[1],
        "w2_words": w2p[0],
        "w2_scales": w2p[1],
        "sg": (np.random.uniform(0.6, 1.6, (R, 1))).astype(np.float32),
        "bg": (np.random.uniform(-1.0, 1.0, (R, 1))).astype(np.float32),
        "wb_words": wbp[0],
        "wb_scales": wbp[1],
        "sx_words": sxp[0],
        "sx_scales": sxp[1],
        "ws_words": wsp[0],
        "ws_scales": wsp[1],
        "offs": striped(idx),
        "offs2": striped(idx2),
        "offs3": striped(idx3),
        "offs4": striped(idx4),
        "offs5": striped(idx5),
    }


def reference(xt_words, xt_scales, w_words, w_scales, w2_words, w2_scales, sg, bg, wb_words, wb_scales, sx_words, sx_scales, ws_words, ws_scales, offs, offs2, offs3, offs4, offs5):
    idx = unstriped(offs)
    idx2 = unstriped(offs2)
    idx3 = unstriped(offs3)
    idx4 = unstriped(offs4)
    idx5 = unstriped(offs5)
    xtu = unpack_weight(xt_words, xt_scales, "e2m1")
    wu = unpack_weight(w_words, w_scales, "e5m2")
    w2u = unpack_weight(w2_words, w2_scales, "e4m3")
    wbu = unpack_weight(wb_words, wb_scales, "e4m3")
    sxu = unpack_weight(sx_words, sx_scales, "e5m2")
    wsu = unpack_weight(ws_words, ws_scales, "e4m3")
    xtidxg = xtu[:, idx]
    a = wu.T @ xtidxg
    xtidx2g = xtu[:, idx2]
    b = w2u.T @ xtidx2g
    hid = b[:, idx4] * sigmoid(a[:, idx3] * f64(sg) + f64(bg))
    hidq = mxq(hid, 0, "e5m2")
    p = wbu.T @ hidq + wsu.T @ sxu
    y = np.zeros((N, E))
    y[:, idx5] = p
    return y

@@ -1,0 +1,165 @@
+from contextlib import ExitStack
+
+import concourse.mybir as mybir
+
+K, T, J, R, O, N, L, E = 512, 2048, 256, 512, 128, 256, 512, 1024
+FLOPS = 2 * (2 * K * R * J + R * N * O + L * N * O)
+
+F32 = mybir.dt.float32
+BF16 = mybir.dt.bfloat16
+I32 = mybir.dt.int32
+U32 = mybir.dt.uint32
+U16 = mybir.dt.uint16
+U8 = mybir.dt.uint8
+E4M3 = mybir.dt.float8_e4m3fn_x4
+E5M2 = mybir.dt.float8_e5m2_x4
+E2M1 = mybir.dt.float4_e2m1fn_x4
+ACT = mybir.ActivationFunctionType
+MULT = mybir.AluOpType.mult
+
+P = 128
+PACK = 4
+
+
+def words_i32(words):
+    return words[0].rearrange("p c t -> p (c t)").bitcast(I32)
+
+
+def load_quadrant(queue, plane, scales, q):
+    queue.dma_start(out=plane[32 * q : 32 * q + 4, :].bitcast(I32), in_=scales[0, 4 * q : 4 * q + 4, :].bitcast(I32))
+
+
+def tile_list_ahead_gatefetch_skip_scattered_kernel(
+    tc, xt_words, xt_scales, w_words, w_scales, w2_words, w2_scales, sg, bg, wb_words, wb_scales,
+    sx_words, sx_scales, ws_words, ws_scales, offs, offs2, offs3, offs4, offs5, out,
+):
+    nc = tc.nc
+    with ExitStack() as ctx:
+        sb = ctx.enter_context(tc.tile_pool(name="sb", bufs=1))
+        shared = ctx.enter_context(tc.tile_pool(name="shared", bufs=1))
+        psum = ctx.enter_context(tc.psum_pool(name="psum", bufs=1))
+
+        list1 = sb.tile([P, J // 16], U16, name="list1")
+        list2 = sb.tile([P, J // 16], U16, name="list2")
+        list3 = sb.tile([P, O // 16], U16, name="list3")
+        list4 = sb.tile([P, O // 16], U16, name="list4")
+        list5 = sb.tile([P, O // 16], U16, name="list5")
+        xt_w = sb.tile([P, T], U16, name="xt_w", align_bytes=64)
+        xt_s = sb.tile([P, T], U8, name="xt_s", align_bytes=64)
+        w_raw = sb.tile([P, R], U32, name="w_raw", align_bytes=64)
+        w2_raw = sb.tile([P, R], U32, name="w2_raw", align_bytes=64)
+        w_s_raw = shared.tile([P, R], U8, name="w_s_raw", offset=0, align_bytes=64)
+        w2_s_raw = sb.tile([P, R], U8, name="w2_s_raw", tag="slot0", align_bytes=64)
+        late = sb.tile([P, 2 * N + O], U8, name="late", align_bytes=64)
+        wb_s = late[:, 0:N]
+        ws_s = late[:, N : 2 * N]
+        sx_s = late[:, 2 * N :]
+        wb_w = sb.tile([P, N], U32, name="wb_w", align_bytes=64)
+        ws_w = sb.tile([P, N], U32, name="ws_w", align_bytes=64)
+        sx_w = sb.tile([P, O], U32, name="sx_w", align_bytes=64)
+        slope = sb.tile([P, PACK], F32, name="slope")
+        shift = sb.tile([P, PACK], F32, name="shift")
+
+        for plane in (w_s_raw, xt_s, w2_s_raw, late):
+            nc.vector.memset(plane[:].bitcast(I32), 0)
+
+        nc.gpsimd.dma_start(out=w_raw[:].bitcast(I32), in_=words_i32(w_words))
+        load_quadrant(nc.gpsimd, w_s_raw, w_scales, 3)
+        nc.gpsimd.dma_start(out=w2_raw[:].bitcast(I32), in_=words_i32(w2_words))
+        nc.gpsimd.dma_start(out=slope[:], in_=sg.rearrange("(p t) one -> p (t one)", t=PACK))
+        nc.gpsimd.dma_start(out=shift[:], in_=bg.rearrange("(p t) one -> p (t one)", t=PACK))
+        nc.gpsimd.dma_start(out=wb_s[0:16, :].bitcast(I32), in_=wb_scales[0].bitcast(I32))
+        nc.sync.dma_start(list1[:], offs)
+        nc.sync.dma_start(list2[:], offs2)
+        nc.sync.dma_start(out=xt_w[:].bitcast(I32), in_=xt_words[0].bitcast(I32))
+        for q in range(4):
+            load_quadrant(nc.scalar, xt_s, xt_scales, q)
+        for q in range(3):
+            load_quadrant(nc.sync, w_s_raw, w_scales, q)
+        for q in range(4):
+            load_quadrant(nc.sync, w2_s_raw, w2_scales, q)
+        nc.sync.dma_start(list3[:], offs3)
+        nc.sync.dma_start(list4[:], offs4)
+        for plane, scales in ((ws_s, ws_scales), (sx_s, sx_scales)):
+            nc.sync.dma_start(out=plane[0:16, :].bitcast(I32), in_=scales[0].bitcast(I32))
+        for tile, words in ((ws_w, ws_words), (sx_w, sx_words), (wb_w, wb_words)):
+            nc.sync.dma_start(out=tile[:].bitcast(I32), in_=words_i32(words))
+        for q in range(1, 4):
+            nc.sync.dma_start(out=late[32 * q : 32 * q + 4, :].bitcast(I32), in_=late[4 * q : 4 * q + 4, :].bitcast(I32))
+        nc.sync.dma_start(list5[:], offs5)
+
+        x1_w = sb.tile([P, J], U16, name="x1_w", align_bytes=64)
+        x1_s = sb.tile([P, J], U8, name="x1_s", align_bytes=64)
+        w_w = sb.tile([P, PACK, P], U32, name="w_w", align_bytes=64)
+        w2_w = sb.tile([P, PACK, P], U32, name="w2_w", align_bytes=64)
+        w_s = sb.tile([P, PACK, P], U8, name="w_s", align_bytes=64)
+        w2_s = sb.tile([P, PACK, P], U8, name="w2_s", tag="slot1", align_bytes=64)
+
+        def deal_words(dealt, raw):
+            nc.scalar.copy(out=dealt[:].rearrange("p t (b i) -> p b t i", i=PACK),
+                           in_=raw[:].rearrange("p (b i t) -> p b t i", i=PACK, t=PACK))
+
+        def deal_bytes(engine, dealt, raw):
+            engine.tensor_copy(out=dealt[:], in_=raw.rearrange("p (m t) -> p t m", t=PACK))
+
+        nc.vector.tensor_copy(out=x1_w[:], in_=xt_w[:].indirect(list1[:]))
+        nc.vector.tensor_copy(out=x1_s[:], in_=xt_s[:].indirect(list1[:]))
+        deal_words(w_w, w_raw)
+        deal_bytes(nc.vector, w_s, w_s_raw[:])
+        x2_s = shared.tile([P, J], U8, name="x2_s", offset=0, align_bytes=64)
+        x2_w = shared.tile([P, J], U16, name="x2_w", offset=J, align_bytes=64)
+        nc.vector.tensor_copy(out=x2_w[:], in_=xt_w[:].indirect(list2[:]))
+        nc.vector.tensor_copy(out=x2_s[:], in_=xt_s[:].indirect(list2[:]))
+        deal_words(w2_w, w2_raw)
+        deal_bytes(nc.vector, w2_s, w2_s_raw[:])
+
+        a_ps = [psum.tile([P, J], F32, name="a_ps%d" % t, tag="bank%d" % t) for t in range(PACK)]
+        b_ps = [psum.tile([P, J], F32, name="b_ps%d" % t, tag="bank%d" % (PACK + t)) for t in range(PACK)]
+        for t in range(PACK):
+            nc.tensor.matmul_mx(out=a_ps[t][:], lhsT=w_w[:, t, :].bitcast(E5M2), lhsT_scale=w_s[:, t, :],
+                                rhs=x1_w[:].bitcast(E2M1), rhs_scale=x1_s[:], start=True, stop=True)
+        for t in range(PACK):
+            nc.tensor.matmul_mx(out=b_ps[t][:], lhsT=w2_w[:, t, :].bitcast(E4M3), lhsT_scale=w2_s[:, t, :],
+                                rhs=x2_w[:].bitcast(E2M1), rhs_scale=x2_s[:], start=True, stop=True)
+
+        pages = [sb.tile([P, E], F32, name="page%d" % h, tag="slot%d" % h, align_bytes=64) for h in range(N // P)]
+        for page in pages:
+            nc.gpsimd.memset(page[:], 0.0)
+
+        gate = sb.tile([P, PACK, O], F32, name="gate")
+        hid = sb.tile([P, PACK, O], F32, name="hid")
+        a_sb = [sb.tile([P, J], F32, name="a_sb%d" % t) for t in range(PACK)]
+        b_sb = [sb.tile([P, J], F32, name="b_sb%d" % t) for t in range(PACK)]
+        for t in range(PACK):
+            nc.scalar.copy(out=a_sb[t][:], in_=a_ps[t][:])
+        for t in range(PACK):
+            nc.scalar.activation(out=gate[:, t, :], in_=a_sb[t][:].indirect(list3[:]), func=ACT.Sigmoid,
+                                 bias=shift[:, t : t + 1], scale=slope[:, t : t + 1])
+        for t in range(PACK):
+            (nc.vector.tensor_copy if t < 3 else nc.scalar.copy)(out=b_sb[t][:], in_=b_ps[t][:])
+        for t in range(PACK):
+            nc.vector.tensor_tensor(out=hid[:, t, :], in0=b_sb[t][:].indirect(list4[:]), in1=gate[:, t, :], op=MULT)
+
+        hid_bf = sb.tile([P, O, PACK], BF16, name="hid_bf", align_bytes=64)
+        hid_w = sb.tile([P, O], U32, name="hid_w", align_bytes=64)
+        hid_s = sb.tile([P, O], U8, name="hid_s", align_bytes=64)
+        nc.vector.tensor_copy(out=hid_bf[:], in_=hid[:].rearrange("p t o -> p o t"))
+        nc.vector.quantize_mx(out=hid_w[:].bitcast(E5M2), scales=hid_s[:], in_=hid_bf[:].rearrange("p o t -> p (o t)"))
+
+        p_ps = [psum.tile([P, O], F32, name="p_ps%d" % h, tag="bank%d" % h) for h in range(N // P)]
+        for h in range(N // P):
+            cols = slice(P * h, P * (h + 1))
+            nc.tensor.matmul_mx(out=p_ps[h][:], lhsT=ws_w[:, cols].bitcast(E4M3), lhsT_scale=ws_s[:, cols],
+                                rhs=sx_w[:].bitcast(E5M2), rhs_scale=sx_s, start=True, stop=False)
+        for h in range(N // P):
+            cols = slice(P * h, P * (h + 1))
+            nc.tensor.matmul_mx(out=p_ps[h][:], lhsT=wb_w[:, cols].bitcast(E4M3), lhsT_scale=wb_s[:, cols],
+                                rhs=hid_w[:].bitcast(E5M2), rhs_scale=hid_s[:], start=False, stop=True)
+
+        p_sb = [sb.tile([P, O], F32, name="p_sb%d" % h) for h in range(N // P)]
+        nc.vector.tensor_copy(out=p_sb[0][:], in_=p_ps[0][:])
+        nc.vector.tensor_copy(out=pages[0][:].indirect(list5[:]), in_=p_sb[0][:])
+        nc.sync.dma_start(out=out[0:P, :], in_=pages[0][:])
+        nc.scalar.copy(out=p_sb[1][:], in_=p_ps[1][:])
+        nc.scalar.activation(out=pages[1][:].indirect(list5[:]), in_=p_sb[1][:], func=ACT.Copy)
+        nc.scalar.dma_start(out=out[P : 2 * P, :], in_=pages[1][:])

@@ -74,6 +74,10 @@ def tile_list_ahead_gatefetch_skip_scattered_kernel(
         nc.sync.dma_start(out=xt_w[:].bitcast(I32), in_=xt_words[0].bitcast(I32))
         for q in range(4):
             load_quadrant(nc.scalar, xt_s, xt_scales, q)
+        warm_in = sb.tile([P, 1], F32, name="warm_in")
+        warm_out = sb.tile([P, 1], F32, name="warm_out")
+        nc.vector.memset(warm_in[:], 0.0)
+        nc.scalar.activation(out=warm_out[:], in_=warm_in[:], func=ACT.Sigmoid)
         for q in range(3):
             load_quadrant(nc.sync, w_s_raw, w_scales, q)
         for q in range(4):

from contextlib import ExitStack

import concourse.mybir as mybir

K, T, J, R, O, N, L, E = 512, 2048, 256, 512, 128, 256, 512, 1024
FLOPS = 2 * (2 * K * R * J + R * N * O + L * N * O)

F32 = mybir.dt.float32
BF16 = mybir.dt.bfloat16
I32 = mybir.dt.int32
U32 = mybir.dt.uint32
U16 = mybir.dt.uint16
U8 = mybir.dt.uint8
E4M3 = mybir.dt.float8_e4m3fn_x4
E5M2 = mybir.dt.float8_e5m2_x4
E2M1 = mybir.dt.float4_e2m1fn_x4
ACT = mybir.ActivationFunctionType
MULT = mybir.AluOpType.mult

P = 128
PACK = 4


def words_i32(words):
    return words[0].rearrange("p c t -> p (c t)").bitcast(I32)


def load_quadrant(queue, plane, scales, q):
    queue.dma_start(out=plane[32 * q : 32 * q + 4, :].bitcast(I32), in_=scales[0, 4 * q : 4 * q + 4, :].bitcast(I32))


def tile_list_ahead_gatefetch_skip_scattered_kernel(
    tc, xt_words, xt_scales, w_words, w_scales, w2_words, w2_scales, sg, bg, wb_words, wb_scales,
    sx_words, sx_scales, ws_words, ws_scales, offs, offs2, offs3, offs4, offs5, out,
):
    nc = tc.nc
    with ExitStack() as ctx:
        sb = ctx.enter_context(tc.tile_pool(name="sb", bufs=1))
        shared = ctx.enter_context(tc.tile_pool(name="shared", bufs=1))
        psum = ctx.enter_context(tc.psum_pool(name="psum", bufs=1))

        list1 = sb.tile([P, J // 16], U16, name="list1")
        list2 = sb.tile([P, J // 16], U16, name="list2")
        list3 = sb.tile([P, O // 16], U16, name="list3")
        list4 = sb.tile([P, O // 16], U16, name="list4")
        list5 = sb.tile([P, O // 16], U16, name="list5")
        xt_w = sb.tile([P, T], U16, name="xt_w", align_bytes=64)
        xt_s = sb.tile([P, T], U8, name="xt_s", align_bytes=64)
        w_raw = sb.tile([P, R], U32, name="w_raw", align_bytes=64)
        w2_raw = sb.tile([P, R], U32, name="w2_raw", align_bytes=64)
        w_s_raw = shared.tile([P, R], U8, name="w_s_raw", offset=0, align_bytes=64)
        w2_s_raw = sb.tile([P, R], U8, name="w2_s_raw", tag="slot0", align_bytes=64)
        late = sb.tile([P, 2 * N + O], U8, name="late", align_bytes=64)
        wb_s = late[:, 0:N]
        ws_s = late[:, N : 2 * N]
        sx_s = late[:, 2 * N :]
        wb_w = sb.tile([P, N], U32, name="wb_w", align_bytes=64)
        ws_w = sb.tile([P, N], U32, name="ws_w", align_bytes=64)
        sx_w = sb.tile([P, O], U32, name="sx_w", align_bytes=64)
        slope = sb.tile([P, PACK], F32, name="slope")
        shift = sb.tile([P, PACK], F32, name="shift")

        for plane in (w_s_raw, xt_s, w2_s_raw, late):
            nc.vector.memset(plane[:].bitcast(I32), 0)

        nc.gpsimd.dma_start(out=w_raw[:].bitcast(I32), in_=words_i32(w_words))
        load_quadrant(nc.gpsimd, w_s_raw, w_scales, 3)
        nc.gpsimd.dma_start(out=w2_raw[:].bitcast(I32), in_=words_i32(w2_words))
        nc.gpsimd.dma_start(out=slope[:], in_=sg.rearrange("(p t) one -> p (t one)", t=PACK))
        nc.gpsimd.dma_start(out=shift[:], in_=bg.rearrange("(p t) one -> p (t one)", t=PACK))
        nc.gpsimd.dma_start(out=wb_s[0:16, :].bitcast(I32), in_=wb_scales[0].bitcast(I32))
        nc.sync.dma_start(list1[:], offs)
        nc.sync.dma_start(list2[:], offs2)
        nc.sync.dma_start(out=xt_w[:].bitcast(I32), in_=xt_words[0].bitcast(I32))
        for q in range(4):
            load_quadrant(nc.scalar, xt_s, xt_scales, q)
        warm_in = sb.tile([P, 1], F32, name="warm_in")
        warm_out = sb.tile([P, 1], F32, name="warm_out")
        nc.vector.memset(warm_in[:], 0.0)
        nc.scalar.activation(out=warm_out[:], in_=warm_in[:], func=ACT.Sigmoid)
        for q in range(3):
            load_quadrant(nc.sync, w_s_raw, w_scales, q)
        for q in range(4):
            load_quadrant(nc.sync, w2_s_raw, w2_scales, q)
        nc.sync.dma_start(list3[:], offs3)
        nc.sync.dma_start(list4[:], offs4)
        for plane, scales in ((ws_s, ws_scales), (sx_s, sx_scales)):
            nc.sync.dma_start(out=plane[0:16, :].bitcast(I32), in_=scales[0].bitcast(I32))
        for tile, words in ((ws_w, ws_words), (sx_w, sx_words), (wb_w, wb_words)):
            nc.sync.dma_start(out=tile[:].bitcast(I32), in_=words_i32(words))
        for q in range(1, 4):
            nc.sync.dma_start(out=late[32 * q : 32 * q + 4, :].bitcast(I32), in_=late[4 * q : 4 * q + 4, :].bitcast(I32))
        nc.sync.dma_start(list5[:], offs5)

        x1_w = sb.tile([P, J], U16, name="x1_w", align_bytes=64)
        x1_s = sb.tile([P, J], U8, name="x1_s", align_bytes=64)
        w_w = sb.tile([P, PACK, P], U32, name="w_w", align_bytes=64)
        w2_w = sb.tile([P, PACK, P], U32, name="w2_w", align_bytes=64)
        w_s = sb.tile([P, PACK, P], U8, name="w_s", align_bytes=64)
        w2_s = sb.tile([P, PACK, P], U8, name="w2_s", tag="slot1", align_bytes=64)

        def deal_words(dealt, raw):
            nc.scalar.copy(out=dealt[:].rearrange("p t (b i) -> p b t i", i=PACK),
                           in_=raw[:].rearrange("p (b i t) -> p b t i", i=PACK, t=PACK))

        def deal_bytes(engine, dealt, raw):
            engine.tensor_copy(out=dealt[:], in_=raw.rearrange("p (m t) -> p t m", t=PACK))

        nc.vector.tensor_copy(out=x1_w[:], in_=xt_w[:].indirect(list1[:]))
        nc.vector.tensor_copy(out=x1_s[:], in_=xt_s[:].indirect(list1[:]))
        deal_words(w_w, w_raw)
        deal_bytes(nc.vector, w_s, w_s_raw[:])
        x2_s = shared.tile([P, J], U8, name="x2_s", offset=0, align_bytes=64)
        x2_w = shared.tile([P, J], U16, name="x2_w", offset=J, align_bytes=64)
        nc.vector.tensor_copy(out=x2_w[:], in_=xt_w[:].indirect(list2[:]))
        nc.vector.tensor_copy(out=x2_s[:], in_=xt_s[:].indirect(list2[:]))
        deal_words(w2_w, w2_raw)
        deal_bytes(nc.vector, w2_s, w2_s_raw[:])

        a_ps = [psum.tile([P, J], F32, name="a_ps%d" % t, tag="bank%d" % t) for t in range(PACK)]
        b_ps = [psum.tile([P, J], F32, name="b_ps%d" % t, tag="bank%d" % (PACK + t)) for t in range(PACK)]
        for t in range(PACK):
            nc.tensor.matmul_mx(out=a_ps[t][:], lhsT=w_w[:, t, :].bitcast(E5M2), lhsT_scale=w_s[:, t, :],
                                rhs=x1_w[:].bitcast(E2M1), rhs_scale=x1_s[:], start=True, stop=True)
        for t in range(PACK):
            nc.tensor.matmul_mx(out=b_ps[t][:], lhsT=w2_w[:, t, :].bitcast(E4M3), lhsT_scale=w2_s[:, t, :],
                                rhs=x2_w[:].bitcast(E2M1), rhs_scale=x2_s[:], start=True, stop=True)

        pages = [sb.tile([P, E], F32, name="page%d" % h, tag="slot%d" % h, align_bytes=64) for h in range(N // P)]
        for page in pages:
            nc.gpsimd.memset(page[:], 0.0)

        gate = sb.tile([P, PACK, O], F32, name="gate")
        hid = sb.tile([P, PACK, O], F32, name="hid")
        a_sb = [sb.tile([P, J], F32, name="a_sb%d" % t) for t in range(PACK)]
        b_sb = [sb.tile([P, J], F32, name="b_sb%d" % t) for t in range(PACK)]
        for t in range(PACK):
            nc.scalar.copy(out=a_sb[t][:], in_=a_ps[t][:])
        for t in range(PACK):
            nc.scalar.activation(out=gate[:, t, :], in_=a_sb[t][:].indirect(list3[:]), func=ACT.Sigmoid,
                                 bias=shift[:, t : t + 1], scale=slope[:, t : t + 1])
        for t in range(PACK):
            (nc.vector.tensor_copy if t < 3 else nc.scalar.copy)(out=b_sb[t][:], in_=b_ps[t][:])
        for t in range(PACK):
            nc.vector.tensor_tensor(out=hid[:, t, :], in0=b_sb[t][:].indirect(list4[:]), in1=gate[:, t, :], op=MULT)

        hid_bf = sb.tile([P, O, PACK], BF16, name="hid_bf", align_bytes=64)
        hid_w = sb.tile([P, O], U32, name="hid_w", align_bytes=64)
        hid_s = sb.tile([P, O], U8, name="hid_s", align_bytes=64)
        nc.vector.tensor_copy(out=hid_bf[:], in_=hid[:].rearrange("p t o -> p o t"))
        nc.vector.quantize_mx(out=hid_w[:].bitcast(E5M2), scales=hid_s[:], in_=hid_bf[:].rearrange("p o t -> p (o t)"))

        p_ps = [psum.tile([P, O], F32, name="p_ps%d" % h, tag="bank%d" % h) for h in range(N // P)]
        for h in range(N // P):
            cols = slice(P * h, P * (h + 1))
            nc.tensor.matmul_mx(out=p_ps[h][:], lhsT=ws_w[:, cols].bitcast(E4M3), lhsT_scale=ws_s[:, cols],
                                rhs=sx_w[:].bitcast(E5M2), rhs_scale=sx_s, start=True, stop=False)
        for h in range(N // P):
            cols = slice(P * h, P * (h + 1))
            nc.tensor.matmul_mx(out=p_ps[h][:], lhsT=wb_w[:, cols].bitcast(E4M3), lhsT_scale=wb_s[:, cols],
                                rhs=hid_w[:].bitcast(E5M2), rhs_scale=hid_s[:], start=False, stop=True)

        p_sb = [sb.tile([P, O], F32, name="p_sb%d" % h) for h in range(N // P)]
        nc.vector.tensor_copy(out=p_sb[0][:], in_=p_ps[0][:])
        nc.vector.tensor_copy(out=pages[0][:].indirect(list5[:]), in_=p_sb[0][:])
        nc.sync.dma_start(out=out[0:P, :], in_=pages[0][:])
        nc.scalar.copy(out=p_sb[1][:], in_=p_ps[1][:])
        nc.scalar.activation(out=pages[1][:].indirect(list5[:]), in_=p_sb[1][:], func=ACT.Copy)
        nc.scalar.dma_start(out=out[P : 2 * P, :], in_=pages[1][:])
